import numpy as np
import ml_dtypes


def mxq(x, axis, fmt="e4m3"):
    dtype, down = {"e4m3": (ml_dtypes.float8_e4m3fn, 7), "e5m2": (ml_dtypes.float8_e5m2, 14)}[fmt]
    v = np.moveaxis(np.asarray(x, np.float32).astype(ml_dtypes.bfloat16).astype(np.float64), axis, -1)
    blocks = v.reshape(v.shape[:-1] + (-1, 32))
    amax = np.abs(blocks).max(-1, keepdims=True)
    byte = np.maximum(np.where(amax > 0, np.frexp(amax)[1] - 1 + 127, 0) - down, 1)
    scale = np.exp2(byte - 127.0)
    codes = (blocks / scale).astype(np.float32).astype(dtype).astype(np.float64)
    return np.moveaxis((codes * scale).reshape(v.shape), -1, axis)


WIDE = False


def mx_kscale(k):
    if not WIDE:
        return np.ones(k)
    levels = np.array([10, -10, 5, -5, 0])
    if k % 512:
        return np.exp2(np.random.permutation(np.resize(levels, k // 32))).repeat(32)
    a = np.empty((k // 512, 16))
    for p in range(k // 512):
        a[p, :8] = np.random.permutation(np.resize(levels, 8))
        for g in range(8):
            far = levels[np.abs(levels - a[p, g]) >= 10]
            a[p, g + 8] = far[np.random.randint(len(far))]
    return np.exp2(a.ravel()).repeat(32)


def f64(x):
    return np.asarray(x).astype(np.float64)


def striped(idx):
    return np.tile(idx.reshape(-1, 16).T, (8, 1)).astype(np.uint16)


def unstriped(offs):
    return offs[:16].T.reshape(-1).astype(np.int64)


E2M1 = np.array([0.0, 0.5, 1.0, 1.5, 2.0, 3.0, 4.0, 6.0, -0.0, -0.5, -1.0, -1.5, -2.0, -3.0, -4.0, -6.0])


def pack_weight(w, fmt):
    k, n = w.shape
    w = f64(np.asarray(w, np.float32).astype(ml_dtypes.bfloat16)).reshape(k // 32, 32, n)
    amax = np.abs(w).max(1)
    if fmt == "e4m3":
        byte = np.frexp(amax)[1] - 1 + 127 - 7
    else:
        mant, ex = np.frexp(amax / 6.0)
        byte = np.where(mant > 0.5, ex, ex - 1) + 127
    byte = np.clip(np.where(amax > 0, byte, 1), 1, 254)
    scaled = (w * np.exp2(127.0 - byte)[:, None, :]).reshape(k, n).astype(np.float32)
    by_word = np.ascontiguousarray(scaled.reshape(k // 512, 128, 4, n).transpose(0, 1, 3, 2))
    if fmt == "e4m3":
        words = by_word.astype(ml_dtypes.float8_e4m3fn).view(np.uint8)
    else:
        c = by_word.astype(ml_dtypes.float4_e2m1fn).view(np.uint8) & 0xF
        words = (c[..., 0::2] | (c[..., 1::2] << 4)).reshape(k // 512, 128, 2 * n)
    return np.ascontiguousarray(words), np.ascontiguousarray(byte.astype(np.uint8).reshape(k // 512, 16, n))


def unpack_weight(words, scales, fmt):
    g, _, n = scales.shape
    words = np.ascontiguousarray(words).reshape(g, 128, n, -1)
    if fmt == "e4m3":
        vals = words.view(ml_dtypes.float8_e4m3fn).astype(np.float64)
    else:
        nib = np.empty((g, 128, n, 4), np.uint8)
        nib[..., 0::2] = words & 0xF
        nib[..., 1::2] = words >> 4
        vals = E2M1[nib]
    vals = vals * np.repeat(np.exp2(scales.astype(np.float64) - 127.0), 8, axis=1)[..., None]
    return vals.transpose(0, 1, 3, 2).reshape(g * 512, n)


def gelu(v):
    return 0.5 * v * (1.0 + np.tanh(np.sqrt(2.0 / np.pi) * (v + 0.044715 * v**3)))


K, K1, K2, H, T, S, T3, S2, P = 1536, 1024, 512, 1024, 4096, 1024, 2048, 1024, 512

def setup_inputs():
    n = np.random.standard_normal
    s = mx_kscale(K)[:, None]
    u = mx_kscale(H)[:, None]
    d = {}
    d["tab_words"], d["tab_scales"] = pack_weight(n((K, T)) * s, "e4m3")
    d["tab2_words"], d["tab2_scales"] = pack_weight(n((H, T3)) / u / H**0.5, "e4m3")
    d["w1"] = (0.55 * n((K1, H)) / s[:K1] / K**0.5).astype(np.float32)
    d["w4_words"], d["w4_scales"] = pack_weight(0.55 * n((K2, H)) / s[K1:] / K**0.5, "e2m1")
    d["gs"] = (1.5 * np.exp(0.4 * n(H)) * u[:, 0]).astype(np.float32)
    d["gc"] = (0.75 * np.exp(0.4 * n(H)) * u[:, 0]).astype(np.float32)
    d["tol"] = (1.2 * n((S2, P))).astype(np.float32)
    d["offs"] = striped(np.random.permutation(T)[:S])
    d["offs2"] = striped(np.random.permutation(T3)[:S2])
    d["pos1"] = striped(np.random.permutation(S)[:P])
    d["pos2"] = striped(np.random.permutation(S)[:P])
    return d

def reference(tab_words, tab_scales, tab2_words, tab2_scales, w1, w4_words, w4_scales, gs, gc, tol, offs, offs2, pos1, pos2):
    v = unpack_weight(tab_words, tab_scales, "e4m3")[:, unstriped(offs)]
    v2 = unpack_weight(tab2_words, tab2_scales, "e4m3")[:, unstriped(offs2)]
    w4 = unpack_weight(w4_words, w4_scales, "e2m1")
    w1q = mxq(f64(w1), 0, "e4m3")
    ph = w1q.T @ v[:K1] + w4.T @ v[K1:]
    h = np.sin(ph) * f64(gs)[:, None] + np.cos(ph) * f64(gc)[:, None]
    hq = mxq(h, 0, "e4m3")
    e = v2.T @ hq
    return np.maximum(e[:, unstriped(pos1)] + e[:, unstriped(pos2)], f64(tol))

@@ -1,0 +1,341 @@
+import math
+from contextlib import ExitStack
+
+import concourse.mybir as mybir
+
+K, K1, K2, H, T, S, T3, S2, PAIRS = 1536, 1024, 512, 1024, 4096, 1024, 2048, 1024, 512
+FLOPS = 2 * K * H * S + 2 * H * S2 * S
+
+F32 = mybir.dt.float32
+BF16 = mybir.dt.bfloat16
+I32 = mybir.dt.int32
+U32 = mybir.dt.uint32
+U16 = mybir.dt.uint16
+U8 = mybir.dt.uint8
+FP8X4 = mybir.dt.float8_e4m3fn_x4
+FP4X4 = mybir.dt.float4_e2m1fn_x4
+ALU = mybir.AluOpType
+ACT = mybir.ActivationFunctionType
+
+P = 128
+PACK = 4
+KP = P * PACK
+N = 512
+CHUNK = 256
+
+
+def tile_list_chronometer_fault_scores_kernel(
+    tc, tab_words, tab_scales, tab2_words, tab2_scales, w1, w4_words, w4_scales, gs, gc, tol, offs, offs2, pos1, pos2, out
+):
+    nc = tc.nc
+    with ExitStack() as ctx:
+        lists = ctx.enter_context(tc.tile_pool(name="lists", bufs=1))
+        keep = ctx.enter_context(tc.tile_pool(name="keep", bufs=1))
+        work = ctx.enter_context(tc.tile_pool(name="work", bufs=2))
+        psum = ctx.enter_context(tc.psum_pool(name="psum", bufs=1))
+
+        idx = lists.tile([P, S // 16], U16, name="idx")
+        idx2 = lists.tile([P, S2 // 16], U16, name="idx2")
+        p1 = lists.tile([P, PAIRS // 16], U16, name="p1")
+        p2 = lists.tile([P, PAIRS // 16], U16, name="p2")
+
+        v_scale_win = keep.tile([P, T], U8, name="v_scale_win", align_bytes=64)
+        w4_scale_raw = keep.tile([P, H], U8, name="w4_scale_raw", align_bytes=64)
+        v2_scale_win = keep.tile([P, T3], U8, name="v2_scale_win", align_bytes=64)
+        nc.vector.memset(v_scale_win[:].bitcast(I32), 0)
+        nc.gpsimd.memset(w4_scale_raw[:].bitcast(I32), 0)
+        nc.vector.memset(v2_scale_win[:].bitcast(I32), 0)
+        for q in range(4):
+            nc.gpsimd.dma_start(
+                out=v_scale_win[32 * q + 4 : 32 * q + 12, :].bitcast(I32),
+                in_=tab_scales[0:2, 4 * q : 4 * q + 4, :].bitcast(I32),
+            )
+
+        gains = keep.tile([P, 2, 8], F32, name="gains")
+        nc.sync.dma_start(idx[:], offs)
+        nc.sync.dma_start(out=gains[:, 0, :].rearrange("p (b t) -> p b t", t=PACK), in_=gs.rearrange("(b p t) -> p b t", p=P, t=PACK))
+        nc.sync.dma_start(out=gains[:, 1, :].rearrange("p (b t) -> p b t", t=PACK), in_=gc.rearrange("(b p t) -> p b t", p=P, t=PACK))
+        w4_raw = keep.tile([P, 2 * H], U8, name="w4_raw", align_bytes=64)
+        nc.sync.dma_start(out=w4_raw[:].bitcast(I32), in_=w4_words[0].bitcast(I32))
+
+        v_win = []
+        w1_raw = {}
+
+        for a in range(3):
+            v_win.append(keep.tile([P, T], U32, name=f"v_win{a}", tag=f"big{a}", align_bytes=64))
+
+        def load_v(a, c0, c1):
+            words = tab_words[a].rearrange("p t i -> p (t i)").bitcast(I32)
+            nc.sync.dma_start(out=v_win[a][:, c0:c1].bitcast(I32), in_=words[:, c0:c1])
+
+        def load_w1(a, b):
+            raw = keep.tile([P, PACK, N], F32, name=f"w1_raw{a}{b}")
+            nc.sync.dma_start(
+                out=raw[:], in_=w1[KP * a : KP * (a + 1), N * b : N * (b + 1)].rearrange("(p j) c -> p j c", j=PACK)
+            )
+            w1_raw[(a, b)] = raw
+
+        def load_w4_scales(q):
+            nc.sync.dma_start(
+                out=w4_scale_raw[32 * q : 32 * q + 4, :].bitcast(I32),
+                in_=w4_scales[0, 4 * q : 4 * q + 4, :].bitcast(I32),
+            )
+
+        load_v(0, 0, T)
+        load_w1(0, 0)
+        for q in range(4):
+            nc.sync.dma_start(
+                out=v_scale_win[32 * q : 32 * q + 4, :].bitcast(I32),
+                in_=tab_scales[2, 4 * q : 4 * q + 4, :].bitcast(I32),
+            )
+        load_w4_scales(0)
+        load_w4_scales(1)
+        load_v(1, 0, T // 2)
+        load_v(1, T // 2, T)
+        load_w4_scales(2)
+        load_w4_scales(3)
+        for q in range(4):
+            nc.sync.dma_start(
+                out=v2_scale_win[32 * q : 32 * q + 8, :].bitcast(I32),
+                in_=tab2_scales[0:2, 4 * q : 4 * q + 4, :].bitcast(I32),
+            )
+        load_w1(1, 0)
+        load_v(2, 0, T // 2)
+        nc.sync.dma_start(idx2[:], offs2)
+        load_v(2, T // 2, T)
+        load_w1(0, 1)
+        load_w1(1, 1)
+        nc.sync.dma_start(p1[:], pos1)
+        nc.sync.dma_start(p2[:], pos2)
+
+        def small(name, width=8):
+            return keep.tile([P, width], F32, name=name)
+
+        g_flat = gains[:].rearrange("p s c -> p (s c)")
+        g_s, g_c = gains[:, 0, :], gains[:, 1, :]
+        half_sign = small("half_sign", 16)
+        nc.vector.tensor_scalar(half_sign[:], g_flat, 0.0, -0.5, ALU.is_ge, ALU.add)
+        half_abs = small("half_abs", 16)
+        nc.vector.tensor_tensor(half_abs[:], g_flat, half_sign[:], ALU.mult)
+        folded = small("folded")
+        nc.vector.tensor_tensor(folded[:], g_s, half_sign[:, 8:16], ALU.mult)
+        norm = small("norm")
+        nc.vector.tensor_tensor(norm[:], half_abs[:, 0:8], half_abs[:, 8:16], ALU.add)
+        safe_norm = small("safe_norm")
+        nc.vector.scalar_tensor_tensor(safe_norm[:], norm[:], 0.0, norm[:], ALU.is_equal, ALU.add)
+        inv_norm = small("inv_norm")
+        nc.vector.reciprocal(inv_norm[:], safe_norm[:])
+        guess = small("guess")
+        nc.vector.scalar_tensor_tensor(guess[:], folded[:], -math.pi / 4.0, inv_norm[:], ALU.mult, ALU.mult)
+        trig = small("trig", 24)
+        sin_half = small("sin_half")
+        nc.scalar.activation(sin_half[:], guess[:], ACT.Sin)
+        nc.scalar.activation(trig[:, 0:8], guess[:], ACT.Sin, scale=-2.0)
+        nc.scalar.activation(trig[:, 16:24], guess[:], ACT.Sin, scale=-2.0)
+        sq_half = small("sq_half")
+        nc.vector.tensor_tensor(sq_half[:], sin_half[:], sin_half[:], ALU.mult)
+        nc.vector.tensor_scalar(trig[:, 8:16], sq_half[:], -2.0, 1.0, ALU.mult, ALU.add)
+        along = small("along", 16)
+        nc.vector.tensor_tensor(along[:], g_flat, trig[:, 0:16], ALU.mult)
+        across = small("across", 16)
+        nc.vector.tensor_tensor(across[:], g_flat, trig[:, 8:24], ALU.mult)
+        r_cos = small("r_cos")
+        nc.vector.tensor_tensor(r_cos[:], along[:, 0:8], along[:, 8:16], ALU.add)
+        r_sin = small("r_sin")
+        nc.vector.tensor_tensor(r_sin[:], across[:, 0:8], across[:, 8:16], ALU.subtract)
+        safe_cos = small("safe_cos")
+        nc.vector.scalar_tensor_tensor(safe_cos[:], norm[:], 0.0, r_cos[:], ALU.is_equal, ALU.add)
+        inv_cos = small("inv_cos")
+        nc.vector.reciprocal(inv_cos[:], safe_cos[:])
+        tan_d = small("tan_d")
+        nc.vector.tensor_tensor(tan_d[:], r_sin[:], inv_cos[:], ALU.mult)
+        tan2 = small("tan2")
+        nc.vector.tensor_tensor(tan2[:], tan_d[:], tan_d[:], ALU.mult)
+        at1, sq1 = small("at1"), small("sq1")
+        nc.vector.tensor_scalar(at1[:], tan2[:], -1.0 / 7.0, 1.0 / 5.0, ALU.mult, ALU.add)
+        nc.vector.tensor_scalar(sq1[:], tan2[:], 1.0 / 16.0, -1.0 / 8.0, ALU.mult, ALU.add)
+        at2, sq2 = small("at2"), small("sq2")
+        nc.vector.tensor_tensor(at2[:], at1[:], tan2[:], ALU.mult)
+        nc.vector.tensor_tensor(sq2[:], sq1[:], tan2[:], ALU.mult)
+        at3, sq3 = small("at3"), small("sq3")
+        nc.vector.scalar_tensor_tensor(at3[:], at2[:], -1.0 / 3.0, tan2[:], ALU.add, ALU.mult)
+        nc.vector.scalar_tensor_tensor(sq3[:], sq2[:], 0.5, tan2[:], ALU.add, ALU.mult)
+        at4, sq4 = small("at4"), small("sq4")
+        nc.vector.scalar_tensor_tensor(at4[:], at3[:], 1.0, tan_d[:], ALU.add, ALU.mult)
+        nc.vector.scalar_tensor_tensor(sq4[:], sq3[:], 1.0, r_cos[:], ALU.add, ALU.mult)
+        shift, amp = small("shift"), small("amp")
+        nc.vector.scalar_tensor_tensor(shift[:], at4[:], -0.5, guess[:], ALU.mult, ALU.add)
+        nc.vector.tensor_scalar(amp[:], sq4[:], -2.0, None, ALU.mult)
+
+        w4_codes = keep.tile([P, 2 * H], U8, name="w4_codes", align_bytes=64)
+        w4_scale = keep.tile([P, H], U8, name="w4_scale", align_bytes=64)
+        nc.vector.tensor_copy(
+            out=w4_codes[:].bitcast(U16).rearrange("p (b t m) -> p b t m", b=2, t=PACK),
+            in_=w4_raw[:].bitcast(U16).rearrange("p (b m t) -> p b t m", b=2, t=PACK),
+        )
+
+        v_codes = {}
+        w1_codes, w1_scale = {}, {}
+
+        def gather_v(a):
+            for h in range(2):
+                g = keep.tile([P, N], U32, name=f"v_codes{a}{h}", align_bytes=64)
+                nc.vector.tensor_copy(g[:], v_win[a][:].indirect(idx[:, 32 * h : 32 * (h + 1)]))
+                v_codes[(a, h)] = g
+
+        def quantise_w1(a, b):
+            dealt = work.tile([P, PACK * N], BF16, name="w1_dealt", align_bytes=64)
+            cast = nc.scalar.copy if b == 0 else nc.vector.tensor_copy
+            cast(
+                out=dealt[:].rearrange("p (t m j) -> p m j t", t=PACK, j=PACK),
+                in_=w1_raw[(a, b)][:].rearrange("p j (m t) -> p m j t", t=PACK),
+            )
+            codes = keep.tile([P, N], U32, name=f"w1_codes{a}{b}", align_bytes=64)
+            scale = keep.tile([P, N], U8, name=f"w1_scale{a}{b}", align_bytes=64)
+            nc.vector.quantize_mx(out=codes[:].bitcast(FP8X4), scales=scale[:], in_=dealt[:])
+            w1_codes[(a, b)], w1_scale[(a, b)] = codes, scale
+
+        gather_v(0)
+        quantise_w1(0, 0)
+        v_scale = keep.tile([P, S], U8, name="v_scale", align_bytes=64)
+        nc.vector.tensor_copy(v_scale[:], v_scale_win[:].indirect(idx[:]))
+        gather_v(1)
+        quantise_w1(1, 0)
+        nc.vector.tensor_copy(
+            out=w4_scale[:].rearrange("p (b t m) -> p b t m", b=2, t=PACK),
+            in_=w4_scale_raw[:].rearrange("p (b m t) -> p b t m", b=2, t=PACK),
+        )
+        v2_scale = keep.tile([P, S2], U8, name="v2_scale", align_bytes=64)
+        nc.vector.tensor_copy(v2_scale[:], v2_scale_win[:].indirect(idx2[:]))
+        gather_v(2)
+
+        v2_win = []
+        for a in range(2):
+            win = keep.tile([P, T3], U32, name=f"v2_win{a}", align_bytes=64)
+            nc.sync.dma_start(out=win[:].bitcast(I32), in_=tab2_words[a].rearrange("p t i -> p (t i)").bitcast(I32))
+            v2_win.append(win)
+        tol_sb = keep.tile([P, S2 // P, PAIRS], F32, name="tol_sb", tag="big0", align_bytes=64)
+        nc.sync.dma_start(out=tol_sb[:], in_=tol.rearrange("(m p) j -> p m j", p=P))
+
+        def ph_pass(bank, a, b, t, h):
+            cols = slice(N * h, N * (h + 1))
+            if a < 2:
+                nc.tensor.matmul_mx(
+                    out=bank[:],
+                    lhsT=w1_codes[(a, b)][:, P * t : P * (t + 1)].bitcast(FP8X4),
+                    lhsT_scale=w1_scale[(a, b)][:, P * t : P * (t + 1)],
+                    rhs=v_codes[(a, h)][:].bitcast(FP8X4),
+                    rhs_scale=v_scale[4 * (a + 1) : P, cols],
+                    start=(a == 0),
+                    stop=False,
+                )
+            else:
+                c0 = N * b + P * t
+                nc.tensor.matmul_mx(
+                    out=bank[:],
+                    lhsT=w4_codes[:, 2 * c0 : 2 * (c0 + P)].bitcast(FP4X4),
+                    lhsT_scale=w4_scale[:, c0 : c0 + P],
+                    rhs=v_codes[(a, h)][:].bitcast(FP8X4),
+                    rhs_scale=v_scale[:, cols],
+                    start=False,
+                    stop=True,
+                )
+
+        h_codes, h_scale = {}, {}
+
+        def make_h(banks, b, h, widths):
+            sines = work.tile([P, PACK, N], F32, name="sines")
+            for t in range(PACK):
+                c = PACK * b + t
+                nc.scalar.activation(sines[:, t, :], banks[t][:], ACT.Sin, bias=shift[:, c : c + 1], scale=0.5)
+            codes = keep.tile([P, N], U32, name=f"h_codes{b}{h}", align_bytes=64)
+            scale = keep.tile([P, N], U8, name=f"h_scale{b}{h}", align_bytes=64)
+            n0 = 0
+            for width in widths:
+                squares = work.tile([P, width, PACK], F32, name="squares", bufs=3)
+                nc.scalar.activation(
+                    squares[:].rearrange("p (c i) t -> p c t i", i=4),
+                    sines[:, :, n0 : n0 + width].rearrange("p t (c i) -> p c t i", i=4),
+                    ACT.Square,
+                )
+                h_bf = work.tile([P, width, PACK], BF16, name="h_bf", align_bytes=64)
+                nc.vector.scalar_tensor_tensor(
+                    h_bf[:],
+                    squares[:],
+                    -0.5,
+                    amp[:, PACK * b : PACK * (b + 1)].unsqueeze(1).to_broadcast([P, width, PACK]),
+                    ALU.add,
+                    ALU.mult,
+                )
+                nc.vector.quantize_mx(
+                    out=codes[:, n0 : n0 + width].bitcast(FP8X4),
+                    scales=scale[:, n0 : n0 + width],
+                    in_=h_bf[:].rearrange("p n t -> p (n t)"),
+                )
+                n0 = n0 + width
+            h_codes[(b, h)], h_scale[(b, h)] = codes, scale
+
+        def new_bank(i):
+            return psum.tile([P, N], F32, name=f"bank{i}", tag=f"bank{i}")
+
+        first = [[new_bank(PACK * h + t) for t in range(PACK)] for h in range(2)]
+        for a in range(3):
+            for h in range(2):
+                for t in range(PACK):
+                    ph_pass(first[h][t], a, 0, t, h)
+        make_h(first[0], 0, 0, (256, 256))
+        quantise_w1(0, 1)
+        quantise_w1(1, 1)
+        make_h(first[1], 0, 1, (256, 256))
+
+        for h in range(2):
+            banks = [new_bank(PACK * h + t) for t in range(PACK)]
+            for t in range(PACK):
+                for a in range(3):
+                    ph_pass(banks[t], a, 1, t, h)
+            make_h(banks, 1, h, (256, 256) if h == 0 else (256, 128, 128))
+
+        v2_codes = {}
+        for half in range(2):
+            entries = idx2[:, 32 * half : 32 * (half + 1)]
+            for a in range(2):
+                g = keep.tile([P, N], U32, name=f"v2_codes{a}{half}", align_bytes=64)
+                nc.vector.tensor_copy(g[:], v2_win[a][:].indirect(entries))
+                v2_codes[(a, half)] = g
+
+        def floor_and_store(summed, m, cols):
+            result = work.tile([P, cols.stop - cols.start], F32, name="result", bufs=3)
+            nc.vector.tensor_tensor(result[:], summed[:], tol_sb[:, m, cols], ALU.max)
+            nc.sync.dma_start(out=out[P * m : P * (m + 1), cols], in_=result[:])
+
+        pending = []
+        for m in range(S2 // P):
+            rows = slice(P * m, P * (m + 1))
+            local = slice(P * (m % PACK), P * (m % PACK + 1))
+            scores = work.tile([P, S], F32, name="scores", bufs=3)
+            for h in range(2):
+                bank = new_bank(PACK * h + m % PACK)
+                for b in range(2):
+                    nc.tensor.matmul_mx(
+                        out=bank[:],
+                        lhsT=v2_codes[(b, m // PACK)][:, local].bitcast(FP8X4),
+                        lhsT_scale=v2_scale[4 * b : P, rows],
+                        rhs=h_codes[(b, h)][:].bitcast(FP8X4),
+                        rhs_scale=h_scale[(b, h)][:],
+                        start=(b == 0),
+                        stop=(b == 1),
+                    )
+                nc.scalar.copy(out=scores[:, N * h : N * (h + 1)], in_=bank[:])
+            pieces = 2 if m == S2 // P - 1 else 1
+            width = PAIRS // pieces
+            for i in range(pieces):
+                cols = slice(width * i, width * (i + 1))
+                entries = slice(width // 16 * i, width // 16 * (i + 1))
+                picked = work.tile([P, width], F32, name="picked")
+                nc.vector.tensor_copy(picked[:], scores[:].indirect(p1[:, entries]))
+                for job in pending:
+                    floor_and_store(*job)
+                summed = work.tile([P, width], F32, name="summed")
+                nc.vector.tensor_tensor(summed[:], scores[:].indirect(p2[:, entries]), picked[:], ALU.add)
+                pending = [(summed, m, cols)]
+        floor_and_store(*pending[0])

@@ -2,6 +2,7 @@ import math
 from contextlib import ExitStack
 
 import concourse.mybir as mybir
+from concourse.masks import make_identity
 
 K, K1, K2, H, T, S, T3, S2, PAIRS = 1536, 1024, 512, 1024, 4096, 1024, 2048, 1024, 512
 FLOPS = 2 * K * H * S + 2 * H * S2 * S
@@ -42,14 +43,22 @@ def tile_list_chronometer_fault_scores_kernel(
         v_scale_win = keep.tile([P, T], U8, name="v_scale_win", align_bytes=64)
         w4_scale_raw = keep.tile([P, H], U8, name="w4_scale_raw", align_bytes=64)
         v2_scale_win = keep.tile([P, T3], U8, name="v2_scale_win", align_bytes=64)
-        nc.vector.memset(v_scale_win[:].bitcast(I32), 0)
-        nc.gpsimd.memset(w4_scale_raw[:].bitcast(I32), 0)
+        nc.gpsimd.memset(v_scale_win[:, 0 : 3 * T // 4].bitcast(I32), 0)
+        nc.vector.memset(v_scale_win[:, 3 * T // 4 : T].bitcast(I32), 0)
+        nc.vector.memset(w4_scale_raw[:].bitcast(I32), 0)
         nc.vector.memset(v2_scale_win[:].bitcast(I32), 0)
-        for q in range(4):
+        for q in range(3):
             nc.gpsimd.dma_start(
                 out=v_scale_win[32 * q + 4 : 32 * q + 12, :].bitcast(I32),
                 in_=tab_scales[0:2, 4 * q : 4 * q + 4, :].bitcast(I32),
             )
+        for q in range(1, 4):
+            nc.gpsimd.dma_start(
+                out=w4_scale_raw[32 * q : 32 * q + 4, :].bitcast(I32),
+                in_=w4_scales[0, 4 * q : 4 * q + 4, :].bitcast(I32),
+            )
+        ident = keep.tile([P, P], F32, name="ident", align_bytes=64)
+        make_identity(nc, ident[:])
 
         gains = keep.tile([P, 2, 8], F32, name="gains")
         nc.sync.dma_start(idx[:], offs)
@@ -57,6 +66,8 @@ def tile_list_chronometer_fault_scores_kernel(
         nc.sync.dma_start(out=gains[:, 1, :].rearrange("p (b t) -> p b t", t=PACK), in_=gc.rearrange("(b p t) -> p b t", p=P, t=PACK))
         w4_raw = keep.tile([P, 2 * H], U8, name="w4_raw", align_bytes=64)
         nc.sync.dma_start(out=w4_raw[:].bitcast(I32), in_=w4_words[0].bitcast(I32))
+        nc.sync.dma_start(idx2[:], offs2)
+        nc.sync.dma_start(p1[:], pos1)
 
         v_win = []
         w1_raw = {}
@@ -69,7 +80,7 @@ def tile_list_chronometer_fault_scores_kernel(
             nc.sync.dma_start(out=v_win[a][:, c0:c1].bitcast(I32), in_=words[:, c0:c1])
 
         def load_w1(a, b):
-            raw = keep.tile([P, PACK, N], F32, name=f"w1_raw{a}{b}")
+            raw = keep.tile([P, PACK, N], F32, name=f"w1_raw{a}{b}", tag=f"w1_raw{a}{b}")
             nc.sync.dma_start(
                 out=raw[:], in_=w1[KP * a : KP * (a + 1), N * b : N * (b + 1)].rearrange("(p j) c -> p j c", j=PACK)
             )
@@ -88,25 +99,25 @@ def tile_list_chronometer_fault_scores_kernel(
                 out=v_scale_win[32 * q : 32 * q + 4, :].bitcast(I32),
                 in_=tab_scales[2, 4 * q : 4 * q + 4, :].bitcast(I32),
             )
-        load_w4_scales(0)
-        load_w4_scales(1)
-        load_v(1, 0, T // 2)
-        load_v(1, T // 2, T)
-        load_w4_scales(2)
-        load_w4_scales(3)
-        for q in range(4):
+        for a in range(2):
             nc.sync.dma_start(
-                out=v2_scale_win[32 * q : 32 * q + 8, :].bitcast(I32),
-                in_=tab2_scales[0:2, 4 * q : 4 * q + 4, :].bitcast(I32),
+                out=v_scale_win[96 + 4 * (a + 1) : 96 + 4 * (a + 2), :].bitcast(I32),
+                in_=tab_scales[a, 12:16, :].bitcast(I32),
             )
         load_w1(1, 0)
+        load_v(1, 0, T // 2)
+        load_w4_scales(0)
+        nc.sync.dma_start(p2[:], pos2)
+        for q in range(4):
+            nc.sync.dma_start(
+                out=v2_scale_win[32 * q + 8 : 32 * q + 16, :].bitcast(I32),
+                in_=tab2_scales[0:2, 4 * q : 4 * q + 4, :].bitcast(I32),
+            )
+        load_v(1, T // 2, T)
         load_v(2, 0, T // 2)
-        nc.sync.dma_start(idx2[:], offs2)
         load_v(2, T // 2, T)
         load_w1(0, 1)
         load_w1(1, 1)
-        nc.sync.dma_start(p1[:], pos1)
-        nc.sync.dma_start(p2[:], pos2)
 
         def small(name, width=8):
             return keep.tile([P, width], F32, name=name)
@@ -185,7 +196,7 @@ def tile_list_chronometer_fault_scores_kernel(
 
         def quantise_w1(a, b):
             dealt = work.tile([P, PACK * N], BF16, name="w1_dealt", align_bytes=64)
-            cast = nc.scalar.copy if b == 0 else nc.vector.tensor_copy
+            cast = nc.vector.tensor_copy if b == 1 else nc.scalar.copy
             cast(
                 out=dealt[:].rearrange("p (t m j) -> p m j t", t=PACK, j=PACK),
                 in_=w1_raw[(a, b)][:].rearrange("p j (m t) -> p m j t", t=PACK),
@@ -199,7 +210,6 @@ def tile_list_chronometer_fault_scores_kernel(
         quantise_w1(0, 0)
         v_scale = keep.tile([P, S], U8, name="v_scale", align_bytes=64)
         nc.vector.tensor_copy(v_scale[:], v_scale_win[:].indirect(idx[:]))
-        gather_v(1)
         quantise_w1(1, 0)
         nc.vector.tensor_copy(
             out=w4_scale[:].rearrange("p (b t m) -> p b t m", b=2, t=PACK),
@@ -207,6 +217,7 @@ def tile_list_chronometer_fault_scores_kernel(
         )
         v2_scale = keep.tile([P, S2], U8, name="v2_scale", align_bytes=64)
         nc.vector.tensor_copy(v2_scale[:], v2_scale_win[:].indirect(idx2[:]))
+        gather_v(1)
         gather_v(2)
 
         v2_win = []
@@ -243,6 +254,13 @@ def tile_list_chronometer_fault_scores_kernel(
 
         h_codes, h_scale = {}, {}
 
+        waiting = []
+
+        def quantise_waiting():
+            for codes, scale, h_bf in waiting:
+                nc.vector.quantize_mx(out=codes.bitcast(FP8X4), scales=scale, in_=h_bf[:].rearrange("p n t -> p (n t)"))
+            waiting.clear()
+
         def make_h(banks, b, h, widths):
             sines = work.tile([P, PACK, N], F32, name="sines")
             for t in range(PACK):
@@ -252,13 +270,13 @@ def tile_list_chronometer_fault_scores_kernel(
             scale = keep.tile([P, N], U8, name=f"h_scale{b}{h}", align_bytes=64)
             n0 = 0
             for width in widths:
-                squares = work.tile([P, width, PACK], F32, name="squares", bufs=3)
+                squares = work.tile([P, width, PACK], F32, name="squares", bufs=4)
                 nc.scalar.activation(
                     squares[:].rearrange("p (c i) t -> p c t i", i=4),
                     sines[:, :, n0 : n0 + width].rearrange("p t (c i) -> p c t i", i=4),
                     ACT.Square,
                 )
-                h_bf = work.tile([P, width, PACK], BF16, name="h_bf", align_bytes=64)
+                h_bf = work.tile([P, width, PACK], BF16, name="h_bf", bufs=3, align_bytes=64)
                 nc.vector.scalar_tensor_tensor(
                     h_bf[:],
                     squares[:],
@@ -267,11 +285,8 @@ def tile_list_chronometer_fault_scores_kernel(
                     ALU.add,
                     ALU.mult,
                 )
-                nc.vector.quantize_mx(
-                    out=codes[:, n0 : n0 + width].bitcast(FP8X4),
-                    scales=scale[:, n0 : n0 + width],
-                    in_=h_bf[:].rearrange("p n t -> p (n t)"),
-                )
+                quantise_waiting()
+                waiting.append((codes[:, n0 : n0 + width], scale[:, n0 : n0 + width], h_bf))
                 n0 = n0 + width
             h_codes[(b, h)], h_scale[(b, h)] = codes, scale
 
@@ -294,6 +309,7 @@ def tile_list_chronometer_fault_scores_kernel(
                 for a in range(3):
                     ph_pass(banks[t], a, 1, t, h)
             make_h(banks, 1, h, (256, 256) if h == 0 else (256, 128, 128))
+        quantise_waiting()
 
         v2_codes = {}
         for half in range(2):
@@ -303,39 +319,82 @@ def tile_list_chronometer_fault_scores_kernel(
                 nc.vector.tensor_copy(g[:], v2_win[a][:].indirect(entries))
                 v2_codes[(a, half)] = g
 
-        def floor_and_store(summed, m, cols):
-            result = work.tile([P, cols.stop - cols.start], F32, name="result", bufs=3)
-            nc.vector.tensor_tensor(result[:], summed[:], tol_sb[:, m, cols], ALU.max)
-            nc.sync.dma_start(out=out[P * m : P * (m + 1), cols], in_=result[:])
+        tiles = S2 // P
+        score_tags = ["w1_raw00", "w1_raw10", "w1_raw01", "w1_raw11"]
 
-        pending = []
-        for m in range(S2 // P):
+        def make_scores(m):
             rows = slice(P * m, P * (m + 1))
             local = slice(P * (m % PACK), P * (m % PACK + 1))
-            scores = work.tile([P, S], F32, name="scores", bufs=3)
-            for h in range(2):
-                bank = new_bank(PACK * h + m % PACK)
+            if m < PACK:
+                scores = work.tile([P, S], F32, name="scores", bufs=PACK)
+            else:
+                scores = keep.tile([P, S], F32, name=f"scores{m}", tag=score_tags[m - PACK])
+            if m == 0:
+                parts = [(0, 0, [(0, 512)]), (2, 1, [(0, 256), (256, 384)]), (3, 1, [(384, 512)])]
+            else:
+                parts = [(m % 2, 0, [(0, 512)]), (2 + m % 2, 1, [(0, 512)])]
+            for bank_no, h, spans in parts:
+                bank = new_bank(bank_no)
+                c0, c1 = spans[0][0], spans[-1][1]
                 for b in range(2):
-                    nc.tensor.matmul_mx(
-                        out=bank[:],
-                        lhsT=v2_codes[(b, m // PACK)][:, local].bitcast(FP8X4),
-                        lhsT_scale=v2_scale[4 * b : P, rows],
-                        rhs=h_codes[(b, h)][:].bitcast(FP8X4),
-                        rhs_scale=h_scale[(b, h)][:],
-                        start=(b == 0),
-                        stop=(b == 1),
-                    )
-                nc.scalar.copy(out=scores[:, N * h : N * (h + 1)], in_=bank[:])
-            pieces = 2 if m == S2 // P - 1 else 1
-            width = PAIRS // pieces
-            for i in range(pieces):
-                cols = slice(width * i, width * (i + 1))
-                entries = slice(width // 16 * i, width // 16 * (i + 1))
-                picked = work.tile([P, width], F32, name="picked")
-                nc.vector.tensor_copy(picked[:], scores[:].indirect(p1[:, entries]))
-                for job in pending:
-                    floor_and_store(*job)
-                summed = work.tile([P, width], F32, name="summed")
-                nc.vector.tensor_tensor(summed[:], scores[:].indirect(p2[:, entries]), picked[:], ALU.add)
-                pending = [(summed, m, cols)]
-        floor_and_store(*pending[0])
+                    for lo, hi in spans:
+                        nc.tensor.matmul_mx(
+                            out=bank[:, lo - c0 : hi - c0],
+                            lhsT=v2_codes[(b, m // PACK)][:, local].bitcast(FP8X4),
+                            lhsT_scale=v2_scale[8 + 4 * b : P, rows],
+                            rhs=h_codes[(b, h)][:, lo:hi].bitcast(FP8X4),
+                            rhs_scale=h_scale[(b, h)][:, lo:hi],
+                            start=(b == 0 and lo == c0),
+                            stop=(b == 1 and hi == c1),
+                        )
+                nc.scalar.copy(out=scores[:, N * h + c0 : N * h + c1], in_=bank[:, 0 : c1 - c0])
+            return scores
+
+        def floor_and_store(summed, m, cols):
+            result = work.tile([P, cols.stop - cols.start], F32, name="result", bufs=3)
+            nc.vector.tensor_tensor(result[:], summed, tol_sb[:, m, cols], ALU.max)
+            nc.sync.dma_start(out=out[P * m : P * (m + 1), cols], in_=result[:])
+
+        def turn_into(bank, source, first, last):
+            for c in range(PACK):
+                cols = slice(P * c, P * (c + 1))
+                nc.tensor.matmul(
+                    bank[:, cols], source[:, cols], ident[:], start=(first and c == 0), stop=(last and c == PACK - 1), is_transpose=True
+                )
+
+        pending = []
+        all_scores = [make_scores(0), make_scores(1)]
+        for m in range(tiles - 1):
+            scores = all_scores[m]
+            turned = new_bank(4 + m % 2)
+            up = work.tile([P, PAIRS], F32, name="up", align_bytes=64)
+            nc.vector.tensor_copy(up[:], scores[:].indirect(p1[:]))
+            turn_into(turned, up, True, False)
+            if len(pending) == 2:
+                floor_and_store(*pending[0])
+                pending = pending[1:]
+            down = work.tile([P, PAIRS], F32, name="down", align_bytes=64)
+            nc.vector.tensor_copy(down[:], scores[:].indirect(p2[:]))
+            turn_into(turned, down, False, True)
+            turned_sum = work.tile([P, PAIRS], F32, name="turned_sum", align_bytes=64)
+            nc.scalar.copy(out=turned_sum[:], in_=turned[:])
+            summed = new_bank(6 + m % 2)
+            turn_into(summed, turned_sum, True, True)
+            pending.append((summed[:], m, slice(0, PAIRS)))
+            for ahead in range(len(all_scores), min(len(all_scores) + 2, tiles)):
+                all_scores.append(make_scores(ahead))
+
+        m = tiles - 1
+        scores = all_scores[m]
+        width = PAIRS // 2
+        for i in range(2):
+            entries = slice(width // 16 * i, width // 16 * (i + 1))
+            up = work.tile([P, width], F32, name="up", align_bytes=64)
+            nc.vector.tensor_copy(up[:], scores[:].indirect(p1[:, entries]))
+            floor_and_store(*pending[0])
+            pending = pending[1:]
+            both = work.tile([P, width], F32, name="down", align_bytes=64)
+            nc.vector.tensor_tensor(both[:], scores[:].indirect(p2[:, entries]), up[:], ALU.add)
+            pending.append((both[:], m, slice(width * i, width * (i + 1))))
+        for job in pending:
+            floor_and_store(*job)

import math
from contextlib import ExitStack

import concourse.mybir as mybir
from concourse.masks import make_identity

K, K1, K2, H, T, S, T3, S2, PAIRS = 1536, 1024, 512, 1024, 4096, 1024, 2048, 1024, 512
FLOPS = 2 * K * H * S + 2 * H * S2 * S

F32 = mybir.dt.float32
BF16 = mybir.dt.bfloat16
I32 = mybir.dt.int32
U32 = mybir.dt.uint32
U16 = mybir.dt.uint16
U8 = mybir.dt.uint8
FP8X4 = mybir.dt.float8_e4m3fn_x4
FP4X4 = mybir.dt.float4_e2m1fn_x4
ALU = mybir.AluOpType
ACT = mybir.ActivationFunctionType

P = 128
PACK = 4
KP = P * PACK
N = 512
CHUNK = 256


def tile_list_chronometer_fault_scores_kernel(
    tc, tab_words, tab_scales, tab2_words, tab2_scales, w1, w4_words, w4_scales, gs, gc, tol, offs, offs2, pos1, pos2, out
):
    nc = tc.nc
    with ExitStack() as ctx:
        lists = ctx.enter_context(tc.tile_pool(name="lists", bufs=1))
        keep = ctx.enter_context(tc.tile_pool(name="keep", bufs=1))
        work = ctx.enter_context(tc.tile_pool(name="work", bufs=2))
        psum = ctx.enter_context(tc.psum_pool(name="psum", bufs=1))

        idx = lists.tile([P, S // 16], U16, name="idx")
        idx2 = lists.tile([P, S2 // 16], U16, name="idx2")
        p1 = lists.tile([P, PAIRS // 16], U16, name="p1")
        p2 = lists.tile([P, PAIRS // 16], U16, name="p2")

        v_scale_win = keep.tile([P, T], U8, name="v_scale_win", align_bytes=64)
        w4_scale_raw = keep.tile([P, H], U8, name="w4_scale_raw", align_bytes=64)
        v2_scale_win = keep.tile([P, T3], U8, name="v2_scale_win", align_bytes=64)
        nc.gpsimd.memset(v_scale_win[:, 0 : 3 * T // 4].bitcast(I32), 0)
        nc.vector.memset(v_scale_win[:, 3 * T // 4 : T].bitcast(I32), 0)
        nc.vector.memset(w4_scale_raw[:].bitcast(I32), 0)
        nc.vector.memset(v2_scale_win[:].bitcast(I32), 0)
        for q in range(3):
            nc.gpsimd.dma_start(
                out=v_scale_win[32 * q + 4 : 32 * q + 12, :].bitcast(I32),
                in_=tab_scales[0:2, 4 * q : 4 * q + 4, :].bitcast(I32),
            )
        for q in range(1, 4):
            nc.gpsimd.dma_start(
                out=w4_scale_raw[32 * q : 32 * q + 4, :].bitcast(I32),
                in_=w4_scales[0, 4 * q : 4 * q + 4, :].bitcast(I32),
            )
        ident = keep.tile([P, P], F32, name="ident", align_bytes=64)
        make_identity(nc, ident[:])

        gains = keep.tile([P, 2, 8], F32, name="gains")
        nc.sync.dma_start(idx[:], offs)
        nc.sync.dma_start(out=gains[:, 0, :].rearrange("p (b t) -> p b t", t=PACK), in_=gs.rearrange("(b p t) -> p b t", p=P, t=PACK))
        nc.sync.dma_start(out=gains[:, 1, :].rearrange("p (b t) -> p b t", t=PACK), in_=gc.rearrange("(b p t) -> p b t", p=P, t=PACK))
        w4_raw = keep.tile([P, 2 * H], U8, name="w4_raw", align_bytes=64)
        nc.sync.dma_start(out=w4_raw[:].bitcast(I32), in_=w4_words[0].bitcast(I32))
        nc.sync.dma_start(idx2[:], offs2)
        nc.sync.dma_start(p1[:], pos1)

        v_win = []
        w1_raw = {}

        for a in range(3):
            v_win.append(keep.tile([P, T], U32, name=f"v_win{a}", tag=f"big{a}", align_bytes=64))

        def load_v(a, c0, c1):
            words = tab_words[a].rearrange("p t i -> p (t i)").bitcast(I32)
            nc.sync.dma_start(out=v_win[a][:, c0:c1].bitcast(I32), in_=words[:, c0:c1])

        def load_w1(a, b):
            raw = keep.tile([P, PACK, N], F32, name=f"w1_raw{a}{b}", tag=f"w1_raw{a}{b}")
            nc.sync.dma_start(
                out=raw[:], in_=w1[KP * a : KP * (a + 1), N * b : N * (b + 1)].rearrange("(p j) c -> p j c", j=PACK)
            )
            w1_raw[(a, b)] = raw

        def load_w4_scales(q):
            nc.sync.dma_start(
                out=w4_scale_raw[32 * q : 32 * q + 4, :].bitcast(I32),
                in_=w4_scales[0, 4 * q : 4 * q + 4, :].bitcast(I32),
            )

        load_v(0, 0, T)
        load_w1(0, 0)
        for q in range(4):
            nc.sync.dma_start(
                out=v_scale_win[32 * q : 32 * q + 4, :].bitcast(I32),
                in_=tab_scales[2, 4 * q : 4 * q + 4, :].bitcast(I32),
            )
        for a in range(2):
            nc.sync.dma_start(
                out=v_scale_win[96 + 4 * (a + 1) : 96 + 4 * (a + 2), :].bitcast(I32),
                in_=tab_scales[a, 12:16, :].bitcast(I32),
            )
        load_w1(1, 0)
        load_v(1, 0, T // 2)
        load_w4_scales(0)
        nc.sync.dma_start(p2[:], pos2)
        for q in range(4):
            nc.sync.dma_start(
                out=v2_scale_win[32 * q + 8 : 32 * q + 16, :].bitcast(I32),
                in_=tab2_scales[0:2, 4 * q : 4 * q + 4, :].bitcast(I32),
            )
        load_v(1, T // 2, T)
        load_v(2, 0, T // 2)
        load_v(2, T // 2, T)
        load_w1(0, 1)
        load_w1(1, 1)

        def small(name, width=8):
            return keep.tile([P, width], F32, name=name)

        g_flat = gains[:].rearrange("p s c -> p (s c)")
        g_s, g_c = gains[:, 0, :], gains[:, 1, :]
        half_sign = small("half_sign", 16)
        nc.vector.tensor_scalar(half_sign[:], g_flat, 0.0, -0.5, ALU.is_ge, ALU.add)
        half_abs = small("half_abs", 16)
        nc.vector.tensor_tensor(half_abs[:], g_flat, half_sign[:], ALU.mult)
        folded = small("folded")
        nc.vector.tensor_tensor(folded[:], g_s, half_sign[:, 8:16], ALU.mult)
        norm = small("norm")
        nc.vector.tensor_tensor(norm[:], half_abs[:, 0:8], half_abs[:, 8:16], ALU.add)
        safe_norm = small("safe_norm")
        nc.vector.scalar_tensor_tensor(safe_norm[:], norm[:], 0.0, norm[:], ALU.is_equal, ALU.add)
        inv_norm = small("inv_norm")
        nc.vector.reciprocal(inv_norm[:], safe_norm[:])
        guess = small("guess")
        nc.vector.scalar_tensor_tensor(guess[:], folded[:], -math.pi / 4.0, inv_norm[:], ALU.mult, ALU.mult)
        trig = small("trig", 24)
        sin_half = small("sin_half")
        nc.scalar.activation(sin_half[:], guess[:], ACT.Sin)
        nc.scalar.activation(trig[:, 0:8], guess[:], ACT.Sin, scale=-2.0)
        nc.scalar.activation(trig[:, 16:24], guess[:], ACT.Sin, scale=-2.0)
        sq_half = small("sq_half")
        nc.vector.tensor_tensor(sq_half[:], sin_half[:], sin_half[:], ALU.mult)
        nc.vector.tensor_scalar(trig[:, 8:16], sq_half[:], -2.0, 1.0, ALU.mult, ALU.add)
        along = small("along", 16)
        nc.vector.tensor_tensor(along[:], g_flat, trig[:, 0:16], ALU.mult)
        across = small("across", 16)
        nc.vector.tensor_tensor(across[:], g_flat, trig[:, 8:24], ALU.mult)
        r_cos = small("r_cos")
        nc.vector.tensor_tensor(r_cos[:], along[:, 0:8], along[:, 8:16], ALU.add)
        r_sin = small("r_sin")
        nc.vector.tensor_tensor(r_sin[:], across[:, 0:8], across[:, 8:16], ALU.subtract)
        safe_cos = small("safe_cos")
        nc.vector.scalar_tensor_tensor(safe_cos[:], norm[:], 0.0, r_cos[:], ALU.is_equal, ALU.add)
        inv_cos = small("inv_cos")
        nc.vector.reciprocal(inv_cos[:], safe_cos[:])
        tan_d = small("tan_d")
        nc.vector.tensor_tensor(tan_d[:], r_sin[:], inv_cos[:], ALU.mult)
        tan2 = small("tan2")
        nc.vector.tensor_tensor(tan2[:], tan_d[:], tan_d[:], ALU.mult)
        at1, sq1 = small("at1"), small("sq1")
        nc.vector.tensor_scalar(at1[:], tan2[:], -1.0 / 7.0, 1.0 / 5.0, ALU.mult, ALU.add)
        nc.vector.tensor_scalar(sq1[:], tan2[:], 1.0 / 16.0, -1.0 / 8.0, ALU.mult, ALU.add)
        at2, sq2 = small("at2"), small("sq2")
        nc.vector.tensor_tensor(at2[:], at1[:], tan2[:], ALU.mult)
        nc.vector.tensor_tensor(sq2[:], sq1[:], tan2[:], ALU.mult)
        at3, sq3 = small("at3"), small("sq3")
        nc.vector.scalar_tensor_tensor(at3[:], at2[:], -1.0 / 3.0, tan2[:], ALU.add, ALU.mult)
        nc.vector.scalar_tensor_tensor(sq3[:], sq2[:], 0.5, tan2[:], ALU.add, ALU.mult)
        at4, sq4 = small("at4"), small("sq4")
        nc.vector.scalar_tensor_tensor(at4[:], at3[:], 1.0, tan_d[:], ALU.add, ALU.mult)
        nc.vector.scalar_tensor_tensor(sq4[:], sq3[:], 1.0, r_cos[:], ALU.add, ALU.mult)
        shift, amp = small("shift"), small("amp")
        nc.vector.scalar_tensor_tensor(shift[:], at4[:], -0.5, guess[:], ALU.mult, ALU.add)
        nc.vector.tensor_scalar(amp[:], sq4[:], -2.0, None, ALU.mult)

        w4_codes = keep.tile([P, 2 * H], U8, name="w4_codes", align_bytes=64)
        w4_scale = keep.tile([P, H], U8, name="w4_scale", align_bytes=64)
        nc.vector.tensor_copy(
            out=w4_codes[:].bitcast(U16).rearrange("p (b t m) -> p b t m", b=2, t=PACK),
            in_=w4_raw[:].bitcast(U16).rearrange("p (b m t) -> p b t m", b=2, t=PACK),
        )

        v_codes = {}
        w1_codes, w1_scale = {}, {}

        def gather_v(a):
            for h in range(2):
                g = keep.tile([P, N], U32, name=f"v_codes{a}{h}", align_bytes=64)
                nc.vector.tensor_copy(g[:], v_win[a][:].indirect(idx[:, 32 * h : 32 * (h + 1)]))
                v_codes[(a, h)] = g

        def quantise_w1(a, b):
            dealt = work.tile([P, PACK * N], BF16, name="w1_dealt", align_bytes=64)
            cast = nc.vector.tensor_copy if b == 1 else nc.scalar.copy
            cast(
                out=dealt[:].rearrange("p (t m j) -> p m j t", t=PACK, j=PACK),
                in_=w1_raw[(a, b)][:].rearrange("p j (m t) -> p m j t", t=PACK),
            )
            codes = keep.tile([P, N], U32, name=f"w1_codes{a}{b}", align_bytes=64)
            scale = keep.tile([P, N], U8, name=f"w1_scale{a}{b}", align_bytes=64)
            nc.vector.quantize_mx(out=codes[:].bitcast(FP8X4), scales=scale[:], in_=dealt[:])
            w1_codes[(a, b)], w1_scale[(a, b)] = codes, scale

        gather_v(0)
        quantise_w1(0, 0)
        v_scale = keep.tile([P, S], U8, name="v_scale", align_bytes=64)
        nc.vector.tensor_copy(v_scale[:], v_scale_win[:].indirect(idx[:]))
        quantise_w1(1, 0)
        nc.vector.tensor_copy(
            out=w4_scale[:].rearrange("p (b t m) -> p b t m", b=2, t=PACK),
            in_=w4_scale_raw[:].rearrange("p (b m t) -> p b t m", b=2, t=PACK),
        )
        v2_scale = keep.tile([P, S2], U8, name="v2_scale", align_bytes=64)
        nc.vector.tensor_copy(v2_scale[:], v2_scale_win[:].indirect(idx2[:]))
        gather_v(1)
        gather_v(2)

        v2_win = []
        for a in range(2):
            win = keep.tile([P, T3], U32, name=f"v2_win{a}", align_bytes=64)
            nc.sync.dma_start(out=win[:].bitcast(I32), in_=tab2_words[a].rearrange("p t i -> p (t i)").bitcast(I32))
            v2_win.append(win)
        tol_sb = keep.tile([P, S2 // P, PAIRS], F32, name="tol_sb", tag="big0", align_bytes=64)
        nc.sync.dma_start(out=tol_sb[:], in_=tol.rearrange("(m p) j -> p m j", p=P))

        def ph_pass(bank, a, b, t, h):
            cols = slice(N * h, N * (h + 1))
            if a < 2:
                nc.tensor.matmul_mx(
                    out=bank[:],
                    lhsT=w1_codes[(a, b)][:, P * t : P * (t + 1)].bitcast(FP8X4),
                    lhsT_scale=w1_scale[(a, b)][:, P * t : P * (t + 1)],
                    rhs=v_codes[(a, h)][:].bitcast(FP8X4),
                    rhs_scale=v_scale[4 * (a + 1) : P, cols],
                    start=(a == 0),
                    stop=False,
                )
            else:
                c0 = N * b + P * t
                nc.tensor.matmul_mx(
                    out=bank[:],
                    lhsT=w4_codes[:, 2 * c0 : 2 * (c0 + P)].bitcast(FP4X4),
                    lhsT_scale=w4_scale[:, c0 : c0 + P],
                    rhs=v_codes[(a, h)][:].bitcast(FP8X4),
                    rhs_scale=v_scale[:, cols],
                    start=False,
                    stop=True,
                )

        h_codes, h_scale = {}, {}

        waiting = []

        def quantise_waiting():
            for codes, scale, h_bf in waiting:
                nc.vector.quantize_mx(out=codes.bitcast(FP8X4), scales=scale, in_=h_bf[:].rearrange("p n t -> p (n t)"))
            waiting.clear()

        def make_h(banks, b, h, widths):
            sines = work.tile([P, PACK, N], F32, name="sines")
            for t in range(PACK):
                c = PACK * b + t
                nc.scalar.activation(sines[:, t, :], banks[t][:], ACT.Sin, bias=shift[:, c : c + 1], scale=0.5)
            codes = keep.tile([P, N], U32, name=f"h_codes{b}{h}", align_bytes=64)
            scale = keep.tile([P, N], U8, name=f"h_scale{b}{h}", align_bytes=64)
            n0 = 0
            for width in widths:
                squares = work.tile([P, width, PACK], F32, name="squares", bufs=4)
                nc.scalar.activation(
                    squares[:].rearrange("p (c i) t -> p c t i", i=4),
                    sines[:, :, n0 : n0 + width].rearrange("p t (c i) -> p c t i", i=4),
                    ACT.Square,
                )
                h_bf = work.tile([P, width, PACK], BF16, name="h_bf", bufs=3, align_bytes=64)
                nc.vector.scalar_tensor_tensor(
                    h_bf[:],
                    squares[:],
                    -0.5,
                    amp[:, PACK * b : PACK * (b + 1)].unsqueeze(1).to_broadcast([P, width, PACK]),
                    ALU.add,
                    ALU.mult,
                )
                quantise_waiting()
                waiting.append((codes[:, n0 : n0 + width], scale[:, n0 : n0 + width], h_bf))
                n0 = n0 + width
            h_codes[(b, h)], h_scale[(b, h)] = codes, scale

        def new_bank(i):
            return psum.tile([P, N], F32, name=f"bank{i}", tag=f"bank{i}")

        first = [[new_bank(PACK * h + t) for t in range(PACK)] for h in range(2)]
        for a in range(3):
            for h in range(2):
                for t in range(PACK):
                    ph_pass(first[h][t], a, 0, t, h)
        make_h(first[0], 0, 0, (256, 256))
        quantise_w1(0, 1)
        quantise_w1(1, 1)
        make_h(first[1], 0, 1, (256, 256))

        for h in range(2):
            banks = [new_bank(PACK * h + t) for t in range(PACK)]
            for t in range(PACK):
                for a in range(3):
                    ph_pass(banks[t], a, 1, t, h)
            make_h(banks, 1, h, (256, 256) if h == 0 else (256, 128, 128))
        quantise_waiting()

        v2_codes = {}
        for half in range(2):
            entries = idx2[:, 32 * half : 32 * (half + 1)]
            for a in range(2):
                g = keep.tile([P, N], U32, name=f"v2_codes{a}{half}", align_bytes=64)
                nc.vector.tensor_copy(g[:], v2_win[a][:].indirect(entries))
                v2_codes[(a, half)] = g

        tiles = S2 // P
        score_tags = ["w1_raw00", "w1_raw10", "w1_raw01", "w1_raw11"]

        def make_scores(m):
            rows = slice(P * m, P * (m + 1))
            local = slice(P * (m % PACK), P * (m % PACK + 1))
            if m < PACK:
                scores = work.tile([P, S], F32, name="scores", bufs=PACK)
            else:
                scores = keep.tile([P, S], F32, name=f"scores{m}", tag=score_tags[m - PACK])
            if m == 0:
                parts = [(0, 0, [(0, 512)]), (2, 1, [(0, 256), (256, 384)]), (3, 1, [(384, 512)])]
            else:
                parts = [(m % 2, 0, [(0, 512)]), (2 + m % 2, 1, [(0, 512)])]
            for bank_no, h, spans in parts:
                bank = new_bank(bank_no)
                c0, c1 = spans[0][0], spans[-1][1]
                for b in range(2):
                    for lo, hi in spans:
                        nc.tensor.matmul_mx(
                            out=bank[:, lo - c0 : hi - c0],
                            lhsT=v2_codes[(b, m // PACK)][:, local].bitcast(FP8X4),
                            lhsT_scale=v2_scale[8 + 4 * b : P, rows],
                            rhs=h_codes[(b, h)][:, lo:hi].bitcast(FP8X4),
                            rhs_scale=h_scale[(b, h)][:, lo:hi],
                            start=(b == 0 and lo == c0),
                            stop=(b == 1 and hi == c1),
                        )
                nc.scalar.copy(out=scores[:, N * h + c0 : N * h + c1], in_=bank[:, 0 : c1 - c0])
            return scores

        def floor_and_store(summed, m, cols):
            result = work.tile([P, cols.stop - cols.start], F32, name="result", bufs=3)
            nc.vector.tensor_tensor(result[:], summed, tol_sb[:, m, cols], ALU.max)
            nc.sync.dma_start(out=out[P * m : P * (m + 1), cols], in_=result[:])

        def turn_into(bank, source, first, last):
            for c in range(PACK):
                cols = slice(P * c, P * (c + 1))
                nc.tensor.matmul(
                    bank[:, cols], source[:, cols], ident[:], start=(first and c == 0), stop=(last and c == PACK - 1), is_transpose=True
                )

        pending = []
        all_scores = [make_scores(0), make_scores(1)]
        for m in range(tiles - 1):
            scores = all_scores[m]
            turned = new_bank(4 + m % 2)
            up = work.tile([P, PAIRS], F32, name="up", align_bytes=64)
            nc.vector.tensor_copy(up[:], scores[:].indirect(p1[:]))
            turn_into(turned, up, True, False)
            if len(pending) == 2:
                floor_and_store(*pending[0])
                pending = pending[1:]
            down = work.tile([P, PAIRS], F32, name="down", align_bytes=64)
            nc.vector.tensor_copy(down[:], scores[:].indirect(p2[:]))
            turn_into(turned, down, False, True)
            turned_sum = work.tile([P, PAIRS], F32, name="turned_sum", align_bytes=64)
            nc.scalar.copy(out=turned_sum[:], in_=turned[:])
            summed = new_bank(6 + m % 2)
            turn_into(summed, turned_sum, True, True)
            pending.append((summed[:], m, slice(0, PAIRS)))
            for ahead in range(len(all_scores), min(len(all_scores) + 2, tiles)):
                all_scores.append(make_scores(ahead))

        m = tiles - 1
        scores = all_scores[m]
        width = PAIRS // 2
        for i in range(2):
            entries = slice(width // 16 * i, width // 16 * (i + 1))
            up = work.tile([P, width], F32, name="up", align_bytes=64)
            nc.vector.tensor_copy(up[:], scores[:].indirect(p1[:, entries]))
            floor_and_store(*pending[0])
            pending = pending[1:]
            both = work.tile([P, width], F32, name="down", align_bytes=64)
            nc.vector.tensor_tensor(both[:], scores[:].indirect(p2[:, entries]), up[:], ALU.add)
            pending.append((both[:], m, slice(width * i, width * (i + 1))))
        for job in pending:
            floor_and_store(*job)
